import numpy as np
CORES = [66,74,82,90,194,202,210,218]
N = 8
TK = 512
EPS = 0.01
GRP = [[0,2,4,5],[1,6],[3,7]]
def setup_inputs(rng):
    return {"x": rng.standard_normal((N, 128, TK), dtype=np.float32) * (0.5 + np.abs(rng.standard_normal((1, 1, TK), dtype=np.float32))) + rng.standard_normal((1, 1, TK), dtype=np.float32)}
def setup_inputs_big(rng):
    d = setup_inputs(rng)
    for k in ("x",): d[k] = (d[k].astype(np.float32) * 1024.0).astype(d[k].dtype)
    return d
def setup_inputs_small(rng):
    d = setup_inputs(rng)
    for k in ("x",): d[k] = (d[k].astype(np.float32) * (1 / 1024.0)).astype(d[k].dtype)
    return d
def setup_inputs_apart(rng):
    d = setup_inputs(rng)
    f = (10.0 ** rng.permutation(np.linspace(-1.5, 1.5, N))).astype(np.float32).reshape(N, 1, 1)
    for k in ("x",): d[k] = (d[k].astype(np.float32) * f).astype(d[k].dtype)
    return d
def setup_inputs_mixed(rng):
    d = setup_inputs(rng)
    f = (10.0 ** rng.uniform(-3, 3, (1, 1, TK))).astype(np.float32); shape = rng.integers(3, size=(1, 1, TK))
    for k in ("x",):
        x = d[k].astype(np.float32)
        m = x.mean(axis=(0, 1), keepdims=True); level = m + np.sign(x - m) * np.abs(x - m).mean(axis=(0, 1), keepdims=True) * rng.uniform(0.9, 1.1, x.shape).astype(np.float32)
        other = x * np.where(rng.random(x.shape) < 0.5, 0.1, 1.0).astype(np.float32)
        d[k] = (np.where(shape == 1, level, np.where(shape == 2, other, x)) * f).astype(d[k].dtype)
    return d
def setup_inputs_offset(rng):
    d = setup_inputs(rng)
    x = d["x"]; spread = x.std(axis=(0, 1), keepdims=True)
    d["x"] = (x + spread * rng.uniform(16, 48, (1, 1, TK)) * rng.choice([-1.0, 1.0], (1, 1, TK))).astype(np.float32)
    return d
def reference(x):
    X = x.astype(np.float64); y = np.zeros_like(X)
    for m in GRP:
        Z = X[m]; D = 128 * len(m)
        Z = Z - Z.sum(axis=(0, 1)) / D
        y[m] = Z / np.sqrt((Z ** 2).sum(axis=(0, 1)) / D + EPS)
    return {"y": y.astype(np.float32)}

@@ -1,0 +1,197 @@
+import math
+from concourse.bass import DstId, RemoteDMATransfer
+from concourse.mybir import AluOpType, AxisListType, ActivationFunctionType
+
+F32 = "float32"
+SCRATCH = {
+    "X": ("sbuf", [128, 4, 4, 32], F32),
+    "Tt": ("sbuf", [128, 512], F32),
+    "J": ("sbuf", [128, 512], F32),
+    "Yt": ("sbuf", [128, 512], F32),
+    "Yn": ("sbuf", [128, 4, 4, 32], F32),
+    "SUM": ("sbuf", [128, 4], F32),
+    "N": ("sbuf", [128, 4], F32),
+    "MSG": ("sbuf", [128, 8], F32),
+    "L": ("sbuf", [128, 24], F32),
+    "OWN": ("sbuf", [128, 24], F32),
+    "DL": ("sbuf", [128, 32], F32),
+    "Q": ("sbuf", [128, 12], F32),
+    "T1": ("sbuf", [128, 16], F32),
+    "T2": ("sbuf", [128, 8], F32),
+    "S2": ("sbuf", [128, 4], F32),
+    "Z": ("sbuf", [128, 4], F32),
+    "SO": ("sbuf", [128, 4], F32),
+    "RO0": ("sbuf", [128, 4], F32),
+    "B1": ("sbuf", [128, 4], F32),
+    "B2": ("sbuf", [128, 4], F32),
+    "CC": ("sbuf", [128, 4], F32),
+    "RO": ("sbuf", [128, 4], F32),
+    "K0": ("sbuf", [128, 4], F32),
+    "K": ("sbuf", [128, 4], F32),
+    "RHO": ("sbuf", [128, 4], F32),
+    "SR": ("sbuf", [128, 4], F32),
+    "RR": ("sbuf", [128, 4], F32),
+    "R1": ("sbuf", [128, 4], F32),
+    "EB": ("sbuf", [128, 4], F32),
+    "NBAR": ("sbuf", [128, 4], F32),
+    "NB": ("sbuf", [128, 4], F32),
+}
+SEMAPHORES = ["ld", "v", "s", "arr", "snt", "st"]
+EPS = 0.01
+NENG = 8
+
+
+def rank_program(g, core, T, topo):
+    rank = T.rank_of(core)
+    if rank is None:
+        return
+    grp = [m for m in T.tables["GRP"] if rank in m][0]
+    G = len(grp)
+    P = G - 1
+    D = 128 * G
+    peers = [q for q in grp if q != rank]
+    sem = T.sem
+    A = AluOpType
+    F = ActivationFunctionType
+    vec, sca, syn = g.vector, g.scalar, g.sync
+    nv, ns = [0], [0]
+
+    def V(inst):
+        inst.then_inc(sem.v, 1)
+        nv[0] += 1
+        return nv[0]
+
+    def S(inst):
+        inst.then_inc(sem.s, 1)
+        ns[0] += 1
+        return ns[0]
+
+    def vdep():
+        vec.wait_ge(sem.v, nv[0])
+
+    def tok(buf, c):
+        return buf[:, 128 * c:128 * c + 128]
+
+    def col(buf, c):
+        return buf[:, c:c + 1]
+
+    for a in range(4):
+        q = syn if a < 2 else sca
+        q.dma_start(T.X[32 * a:32 * a + 32], T.x[:, 128 * a:128 * a + 128]).then_inc(sem.ld, 16)
+
+    V(vec.memset(T.OWN[:, 0:8 * P], 0.0))
+    V(vec.memset(T.DL[:, 8 * P:8 * G], 0.0))
+
+    vec.wait_ge(sem.ld, 64)
+    v_tr = [V(vec.transpose(tok(T.Tt, c), T.X[:, :, c, :])) for c in range(4)]
+
+    v_nm = {}
+    for c in (3, 2):
+        vdep()
+        V(vec.tensor_reduce(col(T.SUM, c), tok(T.Tt, c), AxisListType.X, A.add, negate=True))
+        vdep()
+        v_nm[c] = V(vec.tensor_scalar(col(T.N, c), col(T.SUM, c), 1.0 / 128.0, None, A.mult))
+    s_nm = 0
+    for c in (0, 1):
+        sca.wait_ge(sem.v, v_tr[c])
+        s_nm = S(sca.activation(tok(T.J, c), tok(T.Tt, c), F.Identity, scale=-1.0 / 128.0, accum_out=col(T.N, c)))
+        sca.wait_ge(sem.s, s_nm)
+        S(sca.activation(tok(T.J, c), tok(T.Tt, c), F.Square, bias=col(T.N, c), accum_out=col(T.MSG, 2 * c + 1)))
+    s_sq = 0
+    for c in (3, 2):
+        sca.wait_ge(sem.v, v_nm[c])
+        s_sq = S(sca.activation(tok(T.J, c), tok(T.Tt, c), F.Square, bias=col(T.N, c), accum_out=col(T.MSG, 2 * c + 1)))
+    vdep()
+    vec.wait_ge(sem.s, s_nm)
+    v_a = V(vec.tensor_scalar(T.MSG[:, 0:8:2], T.N[:], math.sqrt(128.0), None, A.mult))
+
+    mask = 0xFFFF
+    for q in peers:
+        mask &= topo.mask(core, T.cores[q])
+    eng = [i for i in range(16) if (mask >> i) & 1][:NENG]
+    emask = sum(1 << i for i in eng)
+    ids, dsts = [], []
+    for q in peers:
+        rid, pid = topo.addr(T.cores[q], core)
+        slot = [m for m in grp if m != q].index(rank)
+        ids.append(DstId(rid=rid, pnc=pid))
+        dsts.append(T.L[:, 8 * slot:8 * slot + 8])
+    g.wait_ge(sem.v, v_a)
+    g.wait_ge(sem.s, s_sq)
+    g.remote_dma_fused([RemoteDMATransfer(dst_ids=ids, dma_engine_mask=emask, remote_sem=sem.arr,
+                                          srcs=[T.MSG[:]], dsts=dsts, alu_op=0)], local_sem=sem.snt)
+    g.wait_ge(sem.snt, len(eng))
+
+    zo = T.DL[:, 8 * P + 1:8 * G:2]
+    vec.wait_ge(sem.s, s_sq)
+    v_zo = V(vec.tensor_scalar(zo, T.MSG[:, 1:8:2], float(D * EPS), None, A.add))
+    sca.wait_ge(sem.v, v_zo)
+    s_so = S(sca.activation(T.SO[:], zo, F.Sqrt, scale=1.0 / D))
+    vdep()
+    for j in range(P):
+        V(vec.tensor_copy(T.OWN[:, 8 * j:8 * j + 8:2], T.MSG[:, 0:8:2]))
+    vec.wait_ge(sem.s, s_so)
+    V(vec.reciprocal(T.RO0[:], T.SO[:]))
+    vdep()
+    V(vec.tensor_tensor(T.B1[:], zo, T.RO0[:], A.mult))
+    vdep()
+    V(vec.tensor_tensor(T.B2[:], T.B1[:], T.RO0[:], A.mult))
+    vdep()
+    V(vec.tensor_scalar(T.CC[:], T.B2[:], -0.5 / D, 1.5, A.mult, A.add))
+    vdep()
+    V(vec.tensor_tensor(T.RO[:], T.RO0[:], T.CC[:], A.mult))
+    vdep()
+    V(vec.tensor_scalar(T.K0[:], T.RO[:], 1.0 / D, None, A.mult))
+    vdep()
+    V(vec.tensor_tensor(T.K[:], T.K0[:], T.RO[:], A.mult))
+
+    vdep()
+    vec.wait_ge(sem.arr, len(eng) * P)
+    V(vec.tensor_tensor(T.DL[:, 0:8 * P], T.L[:, 0:8 * P], T.OWN[:, 0:8 * P], A.subtract))
+    vdep()
+    V(vec.tensor_tensor(T.Q[:, 0:4 * P], T.DL[:, 0:8 * P:2], T.DL[:, 0:8 * P:2], A.mult))
+    vdep()
+    V(vec.tensor_tensor(T.DL[:, 1:8 * P:2], T.DL[:, 1:8 * P:2], T.Q[:, 0:4 * P], A.add))
+    vdep()
+    if G == 4:
+        V(vec.tensor_tensor(T.T1[:], T.DL[:, 0:16], T.DL[:, 16:32], A.add))
+        vdep()
+        v_t2 = V(vec.tensor_tensor(T.T2[:], T.T1[:, 0:8], T.T1[:, 8:16], A.add))
+    else:
+        v_t2 = V(vec.tensor_tensor(T.T2[:], T.DL[:, 0:8], T.DL[:, 8:16], A.add))
+    sca.wait_ge(sem.v, v_t2)
+    s_s2 = S(sca.activation(T.S2[:], T.T2[:, 0:8:2], F.Square, scale=float(G) ** -0.5))
+    vdep()
+    vec.wait_ge(sem.s, s_s2)
+    V(vec.tensor_tensor(T.Z[:], T.T2[:, 1:8:2], T.S2[:], A.subtract))
+    vdep()
+    v_rho = V(vec.tensor_tensor(T.RHO[:], T.Z[:], T.K[:], A.mult))
+    sca.wait_ge(sem.v, v_rho)
+    s_sr = S(sca.activation(T.SR[:], T.RHO[:], F.Sqrt))
+    V(vec.tensor_scalar(T.EB[:], T.T2[:, 0:8:2], 1.0 / (G * math.sqrt(128.0)), None, A.mult))
+    vdep()
+    V(vec.tensor_tensor(T.NBAR[:], T.EB[:], T.N[:], A.add))
+    vec.wait_ge(sem.s, s_sr)
+    V(vec.reciprocal(T.RR[:], T.SR[:]))
+    vdep()
+    V(vec.tensor_tensor(T.R1[:], T.RR[:], T.RO[:], A.mult))
+    vdep()
+    v_nb = V(vec.tensor_tensor(T.NB[:], T.NBAR[:], T.R1[:], A.mult))
+
+    s_y = {}
+    sca.wait_ge(sem.v, v_nb)
+    for c in (0, 1, 2):
+        s_y[c] = S(sca.activation(tok(T.Yt, c), tok(T.Tt, c), F.Identity, bias=col(T.NB, c), scale=col(T.R1, c)))
+    V(vec.tensor_scalar(tok(T.Yt, 3), tok(T.Tt, 3), col(T.NBAR, 3), col(T.R1, 3), A.add, A.mult))
+    vdep()
+    V(vec.transpose(T.Yn[:, :, 3, :], tok(T.Yt, 3)))
+    for c in (0, 1, 2):
+        vec.wait_ge(sem.s, s_y[c])
+        V(vec.transpose(T.Yn[:, :, c, :], tok(T.Yt, c)))
+
+    for a in range(4):
+        q = syn if a < 2 else sca
+        if a % 2 == 0:
+            q.wait_ge(sem.v, nv[0])
+        q.dma_start(T.y[:, 128 * a:128 * a + 128], T.Yn[32 * a:32 * a + 32]).then_inc(sem.st, 16)
+    syn.wait_ge(sem.st, 64)

@@ -7,6 +7,8 @@ SCRATCH = {
     "X": ("sbuf", [128, 4, 4, 32], F32),
     "Tt": ("sbuf", [128, 512], F32),
     "J": ("sbuf", [128, 512], F32),
+    "Dd": ("sbuf", [128, 512], F32),
+    "U": ("sbuf", [128, 512], F32),
     "Yt": ("sbuf", [128, 512], F32),
     "Yn": ("sbuf", [128, 4, 4, 32], F32),
     "SUM": ("sbuf", [128, 4], F32),
@@ -21,22 +23,18 @@ SCRATCH = {
     "S2": ("sbuf", [128, 4], F32),
     "Z": ("sbuf", [128, 4], F32),
     "SO": ("sbuf", [128, 4], F32),
-    "RO0": ("sbuf", [128, 4], F32),
-    "B1": ("sbuf", [128, 4], F32),
-    "B2": ("sbuf", [128, 4], F32),
-    "CC": ("sbuf", [128, 4], F32),
+    "IK": ("sbuf", [128, 4], F32),
+    "KD": ("sbuf", [128, 4], F32),
     "RO": ("sbuf", [128, 4], F32),
     "K0": ("sbuf", [128, 4], F32),
     "K": ("sbuf", [128, 4], F32),
+    "KRO": ("sbuf", [128, 4], F32),
     "RHO": ("sbuf", [128, 4], F32),
     "SR": ("sbuf", [128, 4], F32),
     "RR": ("sbuf", [128, 4], F32),
-    "R1": ("sbuf", [128, 4], F32),
-    "EB": ("sbuf", [128, 4], F32),
-    "NBAR": ("sbuf", [128, 4], F32),
-    "NB": ("sbuf", [128, 4], F32),
+    "NBO": ("sbuf", [128, 4], F32),
 }
-SEMAPHORES = ["ld", "v", "s", "arr", "snt", "st"]
+SEMAPHORES = ["ld0", "ld1", "v", "s", "arr", "snt", "st"]
 EPS = 0.01
 NENG = 8
 
@@ -69,38 +67,41 @@ def rank_program(g, core, T, topo):
     def vdep():
         vec.wait_ge(sem.v, nv[0])
 
+    def sdep():
+        sca.wait_ge(sem.s, ns[0])
+
     def tok(buf, c):
         return buf[:, 128 * c:128 * c + 128]
 
     def col(buf, c):
         return buf[:, c:c + 1]
 
-    for a in range(4):
-        q = syn if a < 2 else sca
-        q.dma_start(T.X[32 * a:32 * a + 32], T.x[:, 128 * a:128 * a + 128]).then_inc(sem.ld, 16)
+    for h in range(2):
+        for a in range(4):
+            q = syn if a < 2 else sca
+            q.dma_start(T.X[32 * a:32 * a + 32, :, 2 * h:2 * h + 2, :],
+                        T.x[:, 128 * a + 64 * h:128 * a + 64 * h + 64]).then_inc(sem["ld%d" % h], 16)
 
     V(vec.memset(T.OWN[:, 0:8 * P], 0.0))
     V(vec.memset(T.DL[:, 8 * P:8 * G], 0.0))
 
-    vec.wait_ge(sem.ld, 64)
-    v_tr = [V(vec.transpose(tok(T.Tt, c), T.X[:, :, c, :])) for c in range(4)]
-
-    v_nm = {}
-    for c in (3, 2):
-        vdep()
-        V(vec.tensor_reduce(col(T.SUM, c), tok(T.Tt, c), AxisListType.X, A.add, negate=True))
-        vdep()
-        v_nm[c] = V(vec.tensor_scalar(col(T.N, c), col(T.SUM, c), 1.0 / 128.0, None, A.mult))
     s_nm = 0
-    for c in (0, 1):
-        sca.wait_ge(sem.v, v_tr[c])
-        s_nm = S(sca.activation(tok(T.J, c), tok(T.Tt, c), F.Identity, scale=-1.0 / 128.0, accum_out=col(T.N, c)))
-        sca.wait_ge(sem.s, s_nm)
-        S(sca.activation(tok(T.J, c), tok(T.Tt, c), F.Square, bias=col(T.N, c), accum_out=col(T.MSG, 2 * c + 1)))
     s_sq = 0
-    for c in (3, 2):
-        sca.wait_ge(sem.v, v_nm[c])
-        s_sq = S(sca.activation(tok(T.J, c), tok(T.Tt, c), F.Square, bias=col(T.N, c), accum_out=col(T.MSG, 2 * c + 1)))
+    for h in range(2):
+        c0, c1 = 2 * h, 2 * h + 1
+        vec.wait_ge(sem["ld%d" % h], 64)
+        v_t0 = V(vec.transpose(tok(T.Tt, c0), T.X[:, :, c0, :]))
+        V(vec.transpose(tok(T.Tt, c1), T.X[:, :, c1, :]))
+        vdep()
+        V(vec.tensor_reduce(col(T.SUM, c1), tok(T.Tt, c1), AxisListType.X, A.add, negate=True))
+        vdep()
+        v_n1 = V(vec.tensor_scalar(col(T.N, c1), col(T.SUM, c1), 1.0 / 128.0, None, A.mult))
+        sca.wait_ge(sem.v, v_t0)
+        s_nm = S(sca.activation(tok(T.J, c0), tok(T.Tt, c0), F.Identity, scale=-1.0 / 128.0, accum_out=col(T.N, c0)))
+        sdep()
+        S(sca.activation(tok(T.J, c0), tok(T.Tt, c0), F.Square, bias=col(T.N, c0), accum_out=col(T.MSG, 2 * c0 + 1)))
+        sca.wait_ge(sem.v, v_n1)
+        s_sq = S(sca.activation(tok(T.J, c1), tok(T.Tt, c1), F.Square, bias=col(T.N, c1), accum_out=col(T.MSG, 2 * c1 + 1)))
     vdep()
     vec.wait_ge(sem.s, s_nm)
     v_a = V(vec.tensor_scalar(T.MSG[:, 0:8:2], T.N[:], math.sqrt(128.0), None, A.mult))
@@ -128,20 +129,22 @@ def rank_program(g, core, T, topo):
     sca.wait_ge(sem.v, v_zo)
     s_so = S(sca.activation(T.SO[:], zo, F.Sqrt, scale=1.0 / D))
     vdep()
+    V(vec.reciprocal(T.IK[:], zo))
+    vdep()
+    V(vec.tensor_scalar(T.KD[:], T.IK[:], float(D), None, A.mult))
     for j in range(P):
         V(vec.tensor_copy(T.OWN[:, 8 * j:8 * j + 8:2], T.MSG[:, 0:8:2]))
+    for c in range(4):
+        V(vec.tensor_scalar(tok(T.Dd, c), tok(T.Tt, c), col(T.N, c), None, A.add))
+    vdep()
     vec.wait_ge(sem.s, s_so)
-    V(vec.reciprocal(T.RO0[:], T.SO[:]))
-    vdep()
-    V(vec.tensor_tensor(T.B1[:], zo, T.RO0[:], A.mult))
-    vdep()
-    V(vec.tensor_tensor(T.B2[:], T.B1[:], T.RO0[:], A.mult))
-    vdep()
-    V(vec.tensor_scalar(T.CC[:], T.B2[:], -0.5 / D, 1.5, A.mult, A.add))
-    vdep()
-    V(vec.tensor_tensor(T.RO[:], T.RO0[:], T.CC[:], A.mult))
+    v_ro = V(vec.tensor_tensor(T.RO[:], T.SO[:], T.KD[:], A.mult))
+    sca.wait_ge(sem.v, v_ro)
+    for c in range(4):
+        S(sca.activation(tok(T.U, c), tok(T.Dd, c), F.Identity, scale=col(T.RO, c)))
     vdep()
     V(vec.tensor_scalar(T.K0[:], T.RO[:], 1.0 / D, None, A.mult))
+    V(vec.tensor_scalar(T.KRO[:], T.RO[:], 1.0 / (G * math.sqrt(128.0)), None, A.mult))
     vdep()
     V(vec.tensor_tensor(T.K[:], T.K0[:], T.RO[:], A.mult))
 
@@ -159,39 +162,52 @@ def rank_program(g, core, T, topo):
         v_t2 = V(vec.tensor_tensor(T.T2[:], T.T1[:, 0:8], T.T1[:, 8:16], A.add))
     else:
         v_t2 = V(vec.tensor_tensor(T.T2[:], T.DL[:, 0:8], T.DL[:, 8:16], A.add))
+    s_u = ns[0]
+    sdep()
     sca.wait_ge(sem.v, v_t2)
     s_s2 = S(sca.activation(T.S2[:], T.T2[:, 0:8:2], F.Square, scale=float(G) ** -0.5))
     vdep()
+    V(vec.tensor_tensor(T.NBO[:], T.T2[:, 0:8:2], T.KRO[:], A.mult))
     vec.wait_ge(sem.s, s_s2)
     V(vec.tensor_tensor(T.Z[:], T.T2[:, 1:8:2], T.S2[:], A.subtract))
     vdep()
     v_rho = V(vec.tensor_tensor(T.RHO[:], T.Z[:], T.K[:], A.mult))
     sca.wait_ge(sem.v, v_rho)
     s_sr = S(sca.activation(T.SR[:], T.RHO[:], F.Sqrt))
-    V(vec.tensor_scalar(T.EB[:], T.T2[:, 0:8:2], 1.0 / (G * math.sqrt(128.0)), None, A.mult))
-    vdep()
-    V(vec.tensor_tensor(T.NBAR[:], T.EB[:], T.N[:], A.add))
+    for c in (0, 1):
+        S(sca.activation(tok(T.U, c), tok(T.U, c), F.Identity, bias=col(T.NBO, c)))
     vec.wait_ge(sem.s, s_sr)
-    V(vec.reciprocal(T.RR[:], T.SR[:]))
-    vdep()
-    V(vec.tensor_tensor(T.R1[:], T.RR[:], T.RO[:], A.mult))
-    vdep()
-    v_nb = V(vec.tensor_tensor(T.NB[:], T.NBAR[:], T.R1[:], A.mult))
+    v_rr = V(vec.reciprocal(T.RR[:], T.SR[:]))
 
     s_y = {}
-    sca.wait_ge(sem.v, v_nb)
-    for c in (0, 1, 2):
-        s_y[c] = S(sca.activation(tok(T.Yt, c), tok(T.Tt, c), F.Identity, bias=col(T.NB, c), scale=col(T.R1, c)))
-    V(vec.tensor_scalar(tok(T.Yt, 3), tok(T.Tt, 3), col(T.NBAR, 3), col(T.R1, 3), A.add, A.mult))
+    sdep()
+    sca.wait_ge(sem.v, v_rr)
+    for c in (0, 1):
+        s_y[c] = S(sca.activation(tok(T.Yt, c), tok(T.U, c), F.Identity, scale=col(T.RR, c)))
+    S(sca.activation(tok(T.U, 3), tok(T.U, 3), F.Identity, bias=col(T.NBO, 3)))
+    sdep()
+    s_y[3] = S(sca.activation(tok(T.Yt, 3), tok(T.U, 3), F.Identity, scale=col(T.RR, 3)))
     vdep()
-    V(vec.transpose(T.Yn[:, :, 3, :], tok(T.Yt, 3)))
-    for c in (0, 1, 2):
+    vec.wait_ge(sem.s, s_u)
+    V(vec.tensor_scalar(tok(T.Yt, 2), tok(T.U, 2), col(T.NBO, 2), col(T.RR, 2), A.add, A.mult))
+    v_h = [0, 0]
+    for c in (0, 1):
         vec.wait_ge(sem.s, s_y[c])
-        V(vec.transpose(T.Yn[:, :, c, :], tok(T.Yt, c)))
+        v_h[0] = V(vec.transpose(T.Yn[:, :, c, :], tok(T.Yt, c)))
+    vdep()
+    V(vec.transpose(T.Yn[:, :, 2, :], tok(T.Yt, 2)))
+    vec.wait_ge(sem.s, s_y[3])
+    v_h[1] = V(vec.transpose(T.Yn[:, :, 3, :], tok(T.Yt, 3)))
 
+    def store(q, a, h):
+        q.dma_start(T.y[:, 128 * a + 64 * h:128 * a + 64 * h + 64],
+                    T.Yn[32 * a:32 * a + 32, :, 2 * h:2 * h + 2, :]).then_inc(sem.st, 16)
+
+    syn.wait_ge(sem.v, v_h[0])
     for a in range(4):
-        q = syn if a < 2 else sca
-        if a % 2 == 0:
-            q.wait_ge(sem.v, nv[0])
-        q.dma_start(T.y[:, 128 * a:128 * a + 128], T.Yn[32 * a:32 * a + 32]).then_inc(sem.st, 16)
-    syn.wait_ge(sem.st, 64)
+        store(syn, a, 0)
+    syn.wait_ge(sem.v, v_h[1])
+    sca.wait_ge(sem.v, v_h[1])
+    for a in range(4):
+        store(syn if a < 2 else sca, a, 1)
+    syn.wait_ge(sem.st, 128)

@@ -14,19 +14,19 @@ SCRATCH = {
     "SUM": ("sbuf", [128, 4], F32),
     "N": ("sbuf", [128, 4], F32),
     "MSG": ("sbuf", [128, 8], F32),
-    "L": ("sbuf", [128, 24], F32),
-    "OWN": ("sbuf", [128, 24], F32),
-    "DL": ("sbuf", [128, 32], F32),
-    "Q": ("sbuf", [128, 12], F32),
+    "L": ("sbuf", [128, 32], F32),
+    "NA": ("sbuf", [128, 4], F32),
+    "JQ": ("sbuf", [128, 16], F32),
+    "SQ": ("sbuf", [128, 4], F32),
     "T1": ("sbuf", [128, 16], F32),
     "T2": ("sbuf", [128, 8], F32),
-    "S2": ("sbuf", [128, 4], F32),
-    "Z": ("sbuf", [128, 4], F32),
+    "ZW": ("sbuf", [128, 4], F32),
+    "P1": ("sbuf", [128, 4], F32),
+    "NB2": ("sbuf", [128, 4], F32),
     "SO": ("sbuf", [128, 4], F32),
     "IK": ("sbuf", [128, 4], F32),
     "KD": ("sbuf", [128, 4], F32),
     "RO": ("sbuf", [128, 4], F32),
-    "K0": ("sbuf", [128, 4], F32),
     "K": ("sbuf", [128, 4], F32),
     "KRO": ("sbuf", [128, 4], F32),
     "RHO": ("sbuf", [128, 4], F32),
@@ -82,9 +82,6 @@ def rank_program(g, core, T, topo):
             q.dma_start(T.X[32 * a:32 * a + 32, :, 2 * h:2 * h + 2, :],
                         T.x[:, 128 * a + 64 * h:128 * a + 64 * h + 64]).then_inc(sem["ld%d" % h], 16)
 
-    V(vec.memset(T.OWN[:, 0:8 * P], 0.0))
-    V(vec.memset(T.DL[:, 8 * P:8 * G], 0.0))
-
     s_nm = 0
     s_sq = 0
     for h in range(2):
@@ -123,55 +120,56 @@ def rank_program(g, core, T, topo):
                                           srcs=[T.MSG[:]], dsts=dsts, alu_op=0)], local_sem=sem.snt)
     g.wait_ge(sem.snt, len(eng))
 
-    zo = T.DL[:, 8 * P + 1:8 * G:2]
+    zo = T.L[:, 8 * P + 1:8 * G:2]
     vec.wait_ge(sem.s, s_sq)
     v_zo = V(vec.tensor_scalar(zo, T.MSG[:, 1:8:2], float(D * EPS), None, A.add))
     sca.wait_ge(sem.v, v_zo)
-    s_so = S(sca.activation(T.SO[:], zo, F.Sqrt, scale=1.0 / D))
+    S(sca.activation(T.SO[:], zo, F.Sqrt, scale=1.0 / D))
     vdep()
+    V(vec.tensor_scalar(T.L[:, 8 * P:8 * G:2], T.MSG[:, 0:8:2], -float(P), None, A.mult))
+    V(vec.tensor_scalar(T.NA[:], T.MSG[:, 0:8:2], -1.0, None, A.mult))
     V(vec.reciprocal(T.IK[:], zo))
     vdep()
     V(vec.tensor_scalar(T.KD[:], T.IK[:], float(D), None, A.mult))
-    for j in range(P):
-        V(vec.tensor_copy(T.OWN[:, 8 * j:8 * j + 8:2], T.MSG[:, 0:8:2]))
+    v_d = 0
     for c in range(4):
-        V(vec.tensor_scalar(tok(T.Dd, c), tok(T.Tt, c), col(T.N, c), None, A.add))
-    vdep()
-    vec.wait_ge(sem.s, s_so)
-    v_ro = V(vec.tensor_tensor(T.RO[:], T.SO[:], T.KD[:], A.mult))
-    sca.wait_ge(sem.v, v_ro)
+        v_d = V(vec.tensor_scalar(tok(T.Dd, c), tok(T.Tt, c), col(T.N, c), None, A.add))
+    sdep()
+    sca.wait_ge(sem.v, v_d)
     for c in range(4):
-        S(sca.activation(tok(T.U, c), tok(T.Dd, c), F.Identity, scale=col(T.RO, c)))
-    vdep()
-    V(vec.tensor_scalar(T.K0[:], T.RO[:], 1.0 / D, None, A.mult))
-    V(vec.tensor_scalar(T.KRO[:], T.RO[:], 1.0 / (G * math.sqrt(128.0)), None, A.mult))
-    vdep()
-    V(vec.tensor_tensor(T.K[:], T.K0[:], T.RO[:], A.mult))
+        S(sca.activation(col(T.RO, c), col(T.SO, c), F.Identity, scale=col(T.KD, c)))
+    sdep()
+    S(sca.activation(T.K[:], T.RO[:], F.Square, scale=float(D) ** -0.5))
+    s_k = S(sca.activation(T.KRO[:], T.RO[:], F.Identity, scale=1.0 / (G * math.sqrt(128.0))))
+    s_u = 0
+    for c in range(4):
+        s_u = S(sca.activation(tok(T.U, c), tok(T.Dd, c), F.Identity, scale=col(T.RO, c)))
 
+    sca.wait_ge(sem.arr, len(eng) * P)
+    s_q = 0
+    for c in range(4):
+        s_q = S(sca.activation(T.JQ[:, 4 * c:4 * c + P], T.L[:, 2 * c:8 * P:8], F.Square, bias=col(T.NA, c),
+                               accum_out=col(T.SQ, c)))
     vdep()
     vec.wait_ge(sem.arr, len(eng) * P)
-    V(vec.tensor_tensor(T.DL[:, 0:8 * P], T.L[:, 0:8 * P], T.OWN[:, 0:8 * P], A.subtract))
-    vdep()
-    V(vec.tensor_tensor(T.Q[:, 0:4 * P], T.DL[:, 0:8 * P:2], T.DL[:, 0:8 * P:2], A.mult))
-    vdep()
-    V(vec.tensor_tensor(T.DL[:, 1:8 * P:2], T.DL[:, 1:8 * P:2], T.Q[:, 0:4 * P], A.add))
-    vdep()
     if G == 4:
-        V(vec.tensor_tensor(T.T1[:], T.DL[:, 0:16], T.DL[:, 16:32], A.add))
+        V(vec.tensor_tensor(T.T1[:], T.L[:, 0:16], T.L[:, 16:32], A.add))
         vdep()
-        v_t2 = V(vec.tensor_tensor(T.T2[:], T.T1[:, 0:8], T.T1[:, 8:16], A.add))
+        V(vec.tensor_tensor(T.T2[:], T.T1[:, 0:8], T.T1[:, 8:16], A.add))
     else:
-        v_t2 = V(vec.tensor_tensor(T.T2[:], T.DL[:, 0:8], T.DL[:, 8:16], A.add))
-    s_u = ns[0]
+        V(vec.tensor_tensor(T.T2[:], T.L[:, 0:8], T.L[:, 8:16], A.add))
+    vdep()
+    vec.wait_ge(sem.s, s_k)
+    v_nbo = V(vec.tensor_tensor(T.NBO[:], T.T2[:, 0:8:2], T.KRO[:], A.mult))
+    vec.wait_ge(sem.s, s_q)
+    v_zw = V(vec.tensor_tensor(T.ZW[:], T.T2[:, 1:8:2], T.SQ[:], A.add))
+    vec.wait_ge(sem.v, v_nbo)
+    V(vec.tensor_tensor(T.NB2[:], T.NBO[:], T.NBO[:], A.mult))
+    vec.wait_ge(sem.v, v_zw)
+    V(vec.tensor_tensor(T.P1[:], T.ZW[:], T.K[:], A.mult))
+    vdep()
+    v_rho = V(vec.tensor_tensor(T.RHO[:], T.P1[:], T.NB2[:], A.subtract))
     sdep()
-    sca.wait_ge(sem.v, v_t2)
-    s_s2 = S(sca.activation(T.S2[:], T.T2[:, 0:8:2], F.Square, scale=float(G) ** -0.5))
-    vdep()
-    V(vec.tensor_tensor(T.NBO[:], T.T2[:, 0:8:2], T.KRO[:], A.mult))
-    vec.wait_ge(sem.s, s_s2)
-    V(vec.tensor_tensor(T.Z[:], T.T2[:, 1:8:2], T.S2[:], A.subtract))
-    vdep()
-    v_rho = V(vec.tensor_tensor(T.RHO[:], T.Z[:], T.K[:], A.mult))
     sca.wait_ge(sem.v, v_rho)
     s_sr = S(sca.activation(T.SR[:], T.RHO[:], F.Sqrt))
     for c in (0, 1):

@@ -31,7 +31,7 @@ SCRATCH = {
     "KRO": ("sbuf", [128, 4], F32),
     "RHO": ("sbuf", [128, 4], F32),
     "SR": ("sbuf", [128, 4], F32),
-    "RR": ("sbuf", [128, 4], F32),
+    "IR": ("sbuf", [128, 4], F32),
     "NBO": ("sbuf", [128, 4], F32),
 }
 SEMAPHORES = ["ld0", "ld1", "v", "s", "arr", "snt", "st"]
@@ -76,31 +76,44 @@ def rank_program(g, core, T, topo):
     def col(buf, c):
         return buf[:, c:c + 1]
 
+    def s_mean(c):
+        return S(sca.activation(tok(T.J, c), tok(T.Tt, c), F.Identity, scale=-1.0 / 128.0, accum_out=col(T.N, c)))
+
+    def s_square(c):
+        return S(sca.activation(tok(T.J, c), tok(T.Tt, c), F.Square, bias=col(T.N, c), accum_out=col(T.MSG, 2 * c + 1)))
+
     for h in range(2):
         for a in range(4):
             q = syn if a < 2 else sca
             q.dma_start(T.X[32 * a:32 * a + 32, :, 2 * h:2 * h + 2, :],
                         T.x[:, 128 * a + 64 * h:128 * a + 64 * h + 64]).then_inc(sem["ld%d" % h], 16)
 
-    s_nm = 0
-    s_sq = 0
-    for h in range(2):
-        c0, c1 = 2 * h, 2 * h + 1
-        vec.wait_ge(sem["ld%d" % h], 64)
-        v_t0 = V(vec.transpose(tok(T.Tt, c0), T.X[:, :, c0, :]))
-        V(vec.transpose(tok(T.Tt, c1), T.X[:, :, c1, :]))
-        vdep()
-        V(vec.tensor_reduce(col(T.SUM, c1), tok(T.Tt, c1), AxisListType.X, A.add, negate=True))
-        vdep()
-        v_n1 = V(vec.tensor_scalar(col(T.N, c1), col(T.SUM, c1), 1.0 / 128.0, None, A.mult))
-        sca.wait_ge(sem.v, v_t0)
-        s_nm = S(sca.activation(tok(T.J, c0), tok(T.Tt, c0), F.Identity, scale=-1.0 / 128.0, accum_out=col(T.N, c0)))
-        sdep()
-        S(sca.activation(tok(T.J, c0), tok(T.Tt, c0), F.Square, bias=col(T.N, c0), accum_out=col(T.MSG, 2 * c0 + 1)))
-        sca.wait_ge(sem.v, v_n1)
-        s_sq = S(sca.activation(tok(T.J, c1), tok(T.Tt, c1), F.Square, bias=col(T.N, c1), accum_out=col(T.MSG, 2 * c1 + 1)))
+    vec.wait_ge(sem.ld0, 64)
+    v_t0 = V(vec.transpose(tok(T.Tt, 0), T.X[:, :, 0, :]))
+    V(vec.transpose(tok(T.Tt, 1), T.X[:, :, 1, :]))
     vdep()
-    vec.wait_ge(sem.s, s_nm)
+    V(vec.tensor_reduce(col(T.SUM, 1), tok(T.Tt, 1), AxisListType.X, A.add, negate=True))
+    vdep()
+    v_n1 = V(vec.tensor_scalar(col(T.N, 1), col(T.SUM, 1), 1.0 / 128.0, None, A.mult))
+    sca.wait_ge(sem.v, v_t0)
+    s_mean(0)
+    sdep()
+    s_square(0)
+    sca.wait_ge(sem.v, v_n1)
+    s_square(1)
+    vec.wait_ge(sem.ld1, 64)
+    v_t2 = V(vec.transpose(tok(T.Tt, 2), T.X[:, :, 2, :]))
+    v_t3 = V(vec.transpose(tok(T.Tt, 3), T.X[:, :, 3, :]))
+    sca.wait_ge(sem.v, v_t2)
+    s_m2 = s_mean(2)
+    sca.wait_ge(sem.v, v_t3)
+    s_m3 = s_mean(3)
+    sca.wait_ge(sem.s, s_m2)
+    s_square(2)
+    sca.wait_ge(sem.s, s_m3)
+    s_sq = s_square(3)
+    vdep()
+    vec.wait_ge(sem.s, s_m3)
     v_a = V(vec.tensor_scalar(T.MSG[:, 0:8:2], T.N[:], math.sqrt(128.0), None, A.mult))
 
     mask = 0xFFFF
@@ -141,9 +154,8 @@ def rank_program(g, core, T, topo):
     sdep()
     S(sca.activation(T.K[:], T.RO[:], F.Square, scale=float(D) ** -0.5))
     s_k = S(sca.activation(T.KRO[:], T.RO[:], F.Identity, scale=1.0 / (G * math.sqrt(128.0))))
-    s_u = 0
     for c in range(4):
-        s_u = S(sca.activation(tok(T.U, c), tok(T.Dd, c), F.Identity, scale=col(T.RO, c)))
+        S(sca.activation(tok(T.U, c), tok(T.Dd, c), F.Identity, scale=col(T.RO, c)))
 
     sca.wait_ge(sem.arr, len(eng) * P)
     s_q = 0
@@ -170,42 +182,47 @@ def rank_program(g, core, T, topo):
     vdep()
     v_rho = V(vec.tensor_tensor(T.RHO[:], T.P1[:], T.NB2[:], A.subtract))
     sdep()
+    sca.wait_ge(sem.v, v_nbo)
+    for c in (2, 3, 0, 1):
+        S(sca.activation(tok(T.U, c), tok(T.U, c), F.Identity, bias=col(T.NBO, c)))
+
     sca.wait_ge(sem.v, v_rho)
     s_sr = S(sca.activation(T.SR[:], T.RHO[:], F.Sqrt))
-    for c in (0, 1):
-        S(sca.activation(tok(T.U, c), tok(T.U, c), F.Identity, bias=col(T.NBO, c)))
-    vec.wait_ge(sem.s, s_sr)
-    v_rr = V(vec.reciprocal(T.RR[:], T.SR[:]))
-
-    s_y = {}
-    sdep()
-    sca.wait_ge(sem.v, v_rr)
-    for c in (0, 1):
-        s_y[c] = S(sca.activation(tok(T.Yt, c), tok(T.U, c), F.Identity, scale=col(T.RR, c)))
-    S(sca.activation(tok(T.U, 3), tok(T.U, 3), F.Identity, bias=col(T.NBO, 3)))
-    sdep()
-    s_y[3] = S(sca.activation(tok(T.Yt, 3), tok(T.U, 3), F.Identity, scale=col(T.RR, 3)))
     vdep()
-    vec.wait_ge(sem.s, s_u)
-    V(vec.tensor_scalar(tok(T.Yt, 2), tok(T.U, 2), col(T.NBO, 2), col(T.RR, 2), A.add, A.mult))
-    v_h = [0, 0]
+    v_ir = V(vec.reciprocal(T.IR[:], T.RHO[:]))
+
+    sdep()
+    s_e = {}
+    for c in (0, 1):
+        s_e[c] = S(sca.activation(tok(T.U, c), tok(T.U, c), F.Identity, scale=col(T.SR, c)))
+    sca.wait_ge(sem.v, v_ir)
+    s_y = {}
+    for c in (0, 1):
+        sca.wait_ge(sem.s, s_e[c])
+        s_y[c] = S(sca.activation(tok(T.Yt, c), tok(T.U, c), F.Identity, scale=col(T.IR, c)))
+    vdep()
+    vec.wait_ge(sem.s, s_sr)
+    v_y = {}
+    for c in (2, 3):
+        v_y[c] = V(vec.tensor_scalar(tok(T.Yt, c), tok(T.U, c), col(T.SR, c), col(T.IR, c), A.mult, A.mult))
+    v_first = 0
+    for c in (2, 3):
+        vec.wait_ge(sem.v, v_y[c])
+        v_first = V(vec.transpose(T.Yn[:, :, c, :], tok(T.Yt, c)))
+    v_last = 0
     for c in (0, 1):
         vec.wait_ge(sem.s, s_y[c])
-        v_h[0] = V(vec.transpose(T.Yn[:, :, c, :], tok(T.Yt, c)))
-    vdep()
-    V(vec.transpose(T.Yn[:, :, 2, :], tok(T.Yt, 2)))
-    vec.wait_ge(sem.s, s_y[3])
-    v_h[1] = V(vec.transpose(T.Yn[:, :, 3, :], tok(T.Yt, 3)))
+        v_last = V(vec.transpose(T.Yn[:, :, c, :], tok(T.Yt, c)))
 
     def store(q, a, h):
         q.dma_start(T.y[:, 128 * a + 64 * h:128 * a + 64 * h + 64],
                     T.Yn[32 * a:32 * a + 32, :, 2 * h:2 * h + 2, :]).then_inc(sem.st, 16)
 
-    syn.wait_ge(sem.v, v_h[0])
+    syn.wait_ge(sem.v, v_first)
     for a in range(4):
-        store(syn, a, 0)
-    syn.wait_ge(sem.v, v_h[1])
-    sca.wait_ge(sem.v, v_h[1])
+        store(syn, a, 1)
+    syn.wait_ge(sem.v, v_last)
+    sca.wait_ge(sem.v, v_last)
     for a in range(4):
-        store(syn if a < 2 else sca, a, 1)
+        store(syn if a < 2 else sca, a, 0)
     syn.wait_ge(sem.st, 128)

@@ -17,21 +17,18 @@ SCRATCH = {
     "L": ("sbuf", [128, 32], F32),
     "NA": ("sbuf", [128, 4], F32),
     "JQ": ("sbuf", [128, 16], F32),
-    "SQ": ("sbuf", [128, 4], F32),
     "T1": ("sbuf", [128, 16], F32),
-    "T2": ("sbuf", [128, 8], F32),
-    "ZW": ("sbuf", [128, 4], F32),
-    "P1": ("sbuf", [128, 4], F32),
-    "NB2": ("sbuf", [128, 4], F32),
+    "D0": ("sbuf", [128, 20], F32),
+    "D1": ("sbuf", [128, 20], F32),
+    "SC": ("sbuf", [128, 20], F32),
     "SO": ("sbuf", [128, 4], F32),
     "IK": ("sbuf", [128, 4], F32),
     "KD": ("sbuf", [128, 4], F32),
     "RO": ("sbuf", [128, 4], F32),
-    "K": ("sbuf", [128, 4], F32),
     "KRO": ("sbuf", [128, 4], F32),
-    "RHO": ("sbuf", [128, 4], F32),
     "SR": ("sbuf", [128, 4], F32),
     "IR": ("sbuf", [128, 4], F32),
+    "GF": ("sbuf", [128, 4], F32),
     "NBO": ("sbuf", [128, 4], F32),
 }
 SEMAPHORES = ["ld0", "ld1", "v", "s", "arr", "snt", "st"]
@@ -76,11 +73,30 @@ def rank_program(g, core, T, topo):
     def col(buf, c):
         return buf[:, c:c + 1]
 
+    def step(buf, k):
+        return buf[:, k:20:5]
+
     def s_mean(c):
         return S(sca.activation(tok(T.J, c), tok(T.Tt, c), F.Identity, scale=-1.0 / 128.0, accum_out=col(T.N, c)))
 
     def s_square(c):
         return S(sca.activation(tok(T.J, c), tok(T.Tt, c), F.Square, bias=col(T.N, c), accum_out=col(T.MSG, 2 * c + 1)))
+
+    mask = 0xFFFF
+    for q in peers:
+        mask &= topo.mask(core, T.cores[q])
+    eng = [i for i in range(16) if (mask >> i) & 1][:NENG]
+    emask = sum(1 << i for i in eng)
+
+    def send(lo, hi):
+        ids, dsts = [], []
+        for q in peers:
+            rid, pid = topo.addr(T.cores[q], core)
+            slot = [m for m in grp if m != q].index(rank)
+            ids.append(DstId(rid=rid, pnc=pid))
+            dsts.append(T.L[:, 8 * slot + lo:8 * slot + hi])
+        g.remote_dma_fused([RemoteDMATransfer(dst_ids=ids, dma_engine_mask=emask, remote_sem=sem.arr,
+                                              srcs=[T.MSG[:, lo:hi]], dsts=dsts, alu_op=0)], local_sem=sem.snt)
 
     for h in range(2):
         for a in range(4):
@@ -88,19 +104,30 @@ def rank_program(g, core, T, topo):
             q.dma_start(T.X[32 * a:32 * a + 32, :, 2 * h:2 * h + 2, :],
                         T.x[:, 128 * a + 64 * h:128 * a + 64 * h + 64]).then_inc(sem["ld%d" % h], 16)
 
+    V(vec.memset(step(T.D0, 0), 0.0))
+    V(vec.memset(step(T.D0, 2), -1.0 / G))
+    V(vec.memset(step(T.D0, 3), 1.0))
+    V(vec.memset(step(T.D1, 1), 0.0))
+    V(vec.memset(step(T.D1, 4), 0.0))
+
     vec.wait_ge(sem.ld0, 64)
     v_t0 = V(vec.transpose(tok(T.Tt, 0), T.X[:, :, 0, :]))
     V(vec.transpose(tok(T.Tt, 1), T.X[:, :, 1, :]))
+    sca.wait_ge(sem.v, v_t0)
+    s_m0 = s_mean(0)
+    sdep()
+    s_sq0 = s_square(0)
     vdep()
     V(vec.tensor_reduce(col(T.SUM, 1), tok(T.Tt, 1), AxisListType.X, A.add, negate=True))
+    vec.wait_ge(sem.s, s_m0)
+    v_a0 = V(vec.tensor_scalar(col(T.MSG, 0), col(T.N, 0), math.sqrt(128.0), None, A.mult))
     vdep()
     v_n1 = V(vec.tensor_scalar(col(T.N, 1), col(T.SUM, 1), 1.0 / 128.0, None, A.mult))
-    sca.wait_ge(sem.v, v_t0)
-    s_mean(0)
-    sdep()
-    s_square(0)
     sca.wait_ge(sem.v, v_n1)
     s_square(1)
+    g.wait_ge(sem.v, v_a0)
+    g.wait_ge(sem.s, s_sq0)
+    send(0, 2)
     vec.wait_ge(sem.ld1, 64)
     v_t2 = V(vec.transpose(tok(T.Tt, 2), T.X[:, :, 2, :]))
     v_t3 = V(vec.transpose(tok(T.Tt, 3), T.X[:, :, 3, :]))
@@ -114,97 +141,85 @@ def rank_program(g, core, T, topo):
     s_sq = s_square(3)
     vdep()
     vec.wait_ge(sem.s, s_m3)
-    v_a = V(vec.tensor_scalar(T.MSG[:, 0:8:2], T.N[:], math.sqrt(128.0), None, A.mult))
-
-    mask = 0xFFFF
-    for q in peers:
-        mask &= topo.mask(core, T.cores[q])
-    eng = [i for i in range(16) if (mask >> i) & 1][:NENG]
-    emask = sum(1 << i for i in eng)
-    ids, dsts = [], []
-    for q in peers:
-        rid, pid = topo.addr(T.cores[q], core)
-        slot = [m for m in grp if m != q].index(rank)
-        ids.append(DstId(rid=rid, pnc=pid))
-        dsts.append(T.L[:, 8 * slot:8 * slot + 8])
+    v_a = V(vec.tensor_scalar(T.MSG[:, 2:8:2], T.N[:, 1:4], math.sqrt(128.0), None, A.mult))
     g.wait_ge(sem.v, v_a)
     g.wait_ge(sem.s, s_sq)
-    g.remote_dma_fused([RemoteDMATransfer(dst_ids=ids, dma_engine_mask=emask, remote_sem=sem.arr,
-                                          srcs=[T.MSG[:]], dsts=dsts, alu_op=0)], local_sem=sem.snt)
-    g.wait_ge(sem.snt, len(eng))
+    send(2, 8)
+    g.wait_ge(sem.snt, 2 * len(eng))
+    landed = 2 * len(eng) * P
 
     zo = T.L[:, 8 * P + 1:8 * G:2]
+    sdep()
+    S(sca.activation(T.SO[:], T.MSG[:, 1:8:2], F.Sqrt, bias=EPS, scale=1.0 / D))
     vec.wait_ge(sem.s, s_sq)
-    v_zo = V(vec.tensor_scalar(zo, T.MSG[:, 1:8:2], float(D * EPS), None, A.add))
-    sca.wait_ge(sem.v, v_zo)
-    S(sca.activation(T.SO[:], zo, F.Sqrt, scale=1.0 / D))
+    V(vec.tensor_scalar(zo, T.MSG[:, 1:8:2], float(D * EPS), None, A.add))
     vdep()
+    V(vec.reciprocal(T.IK[:], zo))
     V(vec.tensor_scalar(T.L[:, 8 * P:8 * G:2], T.MSG[:, 0:8:2], -float(P), None, A.mult))
     V(vec.tensor_scalar(T.NA[:], T.MSG[:, 0:8:2], -1.0, None, A.mult))
-    V(vec.reciprocal(T.IK[:], zo))
     vdep()
-    V(vec.tensor_scalar(T.KD[:], T.IK[:], float(D), None, A.mult))
-    v_d = 0
+    v_kd = V(vec.tensor_scalar(T.KD[:], T.IK[:], float(D), None, A.mult))
     for c in range(4):
-        v_d = V(vec.tensor_scalar(tok(T.Dd, c), tok(T.Tt, c), col(T.N, c), None, A.add))
+        V(vec.tensor_scalar(tok(T.Dd, c), tok(T.Tt, c), col(T.N, c), None, A.add))
     sdep()
-    sca.wait_ge(sem.v, v_d)
+    sca.wait_ge(sem.v, v_kd)
     for c in range(4):
         S(sca.activation(col(T.RO, c), col(T.SO, c), F.Identity, scale=col(T.KD, c)))
     sdep()
-    S(sca.activation(T.K[:], T.RO[:], F.Square, scale=float(D) ** -0.5))
     s_k = S(sca.activation(T.KRO[:], T.RO[:], F.Identity, scale=1.0 / (G * math.sqrt(128.0))))
-    for c in range(4):
-        S(sca.activation(tok(T.U, c), tok(T.Dd, c), F.Identity, scale=col(T.RO, c)))
+    S(sca.activation(step(T.D0, 4), T.RO[:], F.Square, scale=float(D) ** -0.5))
 
-    sca.wait_ge(sem.arr, len(eng) * P)
+    sca.wait_ge(sem.arr, landed)
     s_q = 0
     for c in range(4):
         s_q = S(sca.activation(T.JQ[:, 4 * c:4 * c + P], T.L[:, 2 * c:8 * P:8], F.Square, bias=col(T.NA, c),
-                               accum_out=col(T.SQ, c)))
+                               accum_out=T.D1[:, 5 * c + 3:5 * c + 4]))
     vdep()
-    vec.wait_ge(sem.arr, len(eng) * P)
+    vec.wait_ge(sem.arr, landed)
     if G == 4:
         V(vec.tensor_tensor(T.T1[:], T.L[:, 0:16], T.L[:, 16:32], A.add))
         vdep()
-        V(vec.tensor_tensor(T.T2[:], T.T1[:, 0:8], T.T1[:, 8:16], A.add))
+        pair = T.T1
     else:
-        V(vec.tensor_tensor(T.T2[:], T.L[:, 0:8], T.L[:, 8:16], A.add))
-    vdep()
+        pair = T.L
+    v_t = V(vec.tensor_tensor(step(T.D1, 0), pair[:, 0:8:2], pair[:, 8:16:2], A.add))
+    V(vec.tensor_tensor(step(T.D0, 1), pair[:, 0:8:2], pair[:, 8:16:2], A.add))
+    V(vec.tensor_tensor(step(T.D1, 2), pair[:, 1:8:2], pair[:, 9:16:2], A.add))
+    vec.wait_ge(sem.v, v_t)
     vec.wait_ge(sem.s, s_k)
-    v_nbo = V(vec.tensor_tensor(T.NBO[:], T.T2[:, 0:8:2], T.KRO[:], A.mult))
+    v_nbo = V(vec.tensor_tensor(T.NBO[:], step(T.D1, 0), T.KRO[:], A.mult))
+    vdep()
     vec.wait_ge(sem.s, s_q)
-    v_zw = V(vec.tensor_tensor(T.ZW[:], T.T2[:, 1:8:2], T.SQ[:], A.add))
-    vec.wait_ge(sem.v, v_nbo)
-    V(vec.tensor_tensor(T.NB2[:], T.NBO[:], T.NBO[:], A.mult))
-    vec.wait_ge(sem.v, v_zw)
-    V(vec.tensor_tensor(T.P1[:], T.ZW[:], T.K[:], A.mult))
-    vdep()
-    v_rho = V(vec.tensor_tensor(T.RHO[:], T.P1[:], T.NB2[:], A.subtract))
-    sdep()
+    v_rho = V(vec.tensor_tensor_scan(T.SC[:], T.D0[:], T.D1[:], 0.0, A.mult, A.add))
+    rho = step(T.SC, 4)
+
+    def s_w(c):
+        return S(sca.activation(tok(T.U, c), tok(T.Dd, c), F.Identity, bias=col(T.NBO, c), scale=col(T.RO, c)))
+
     sca.wait_ge(sem.v, v_nbo)
-    for c in (2, 3, 0, 1):
-        S(sca.activation(tok(T.U, c), tok(T.U, c), F.Identity, bias=col(T.NBO, c)))
-
+    s_w(2)
     sca.wait_ge(sem.v, v_rho)
-    s_sr = S(sca.activation(T.SR[:], T.RHO[:], F.Sqrt))
+    s_sr = S(sca.activation(T.SR[:], rho, F.Sqrt))
+    s_w3 = s_w(3)
+    s_w(0)
+    s_w(1)
     vdep()
-    v_ir = V(vec.reciprocal(T.IR[:], T.RHO[:]))
+    v_ir = V(vec.reciprocal(T.IR[:], rho))
 
     sdep()
-    s_e = {}
-    for c in (0, 1):
-        s_e[c] = S(sca.activation(tok(T.U, c), tok(T.U, c), F.Identity, scale=col(T.SR, c)))
     sca.wait_ge(sem.v, v_ir)
+    for c in (0, 1):
+        S(sca.activation(col(T.GF, c), col(T.SR, c), F.Identity, scale=col(T.IR, c)))
+    sdep()
     s_y = {}
     for c in (0, 1):
-        sca.wait_ge(sem.s, s_e[c])
-        s_y[c] = S(sca.activation(tok(T.Yt, c), tok(T.U, c), F.Identity, scale=col(T.IR, c)))
+        s_y[c] = S(sca.activation(tok(T.Yt, c), tok(T.U, c), F.Identity, scale=col(T.GF, c)))
     vdep()
     vec.wait_ge(sem.s, s_sr)
     v_y = {}
-    for c in (2, 3):
-        v_y[c] = V(vec.tensor_scalar(tok(T.Yt, c), tok(T.U, c), col(T.SR, c), col(T.IR, c), A.mult, A.mult))
+    v_y[2] = V(vec.tensor_scalar(tok(T.Yt, 2), tok(T.U, 2), col(T.SR, 2), col(T.IR, 2), A.mult, A.mult))
+    vec.wait_ge(sem.s, s_w3)
+    v_y[3] = V(vec.tensor_scalar(tok(T.Yt, 3), tok(T.U, 3), col(T.SR, 3), col(T.IR, 3), A.mult, A.mult))
     v_first = 0
     for c in (2, 3):
         vec.wait_ge(sem.v, v_y[c])

import math
from concourse.bass import DstId, RemoteDMATransfer
from concourse.mybir import AluOpType, AxisListType, ActivationFunctionType

F32 = "float32"
SCRATCH = {
    "X": ("sbuf", [128, 4, 4, 32], F32),
    "Tt": ("sbuf", [128, 512], F32),
    "J": ("sbuf", [128, 512], F32),
    "Dd": ("sbuf", [128, 512], F32),
    "U": ("sbuf", [128, 512], F32),
    "Yt": ("sbuf", [128, 512], F32),
    "Yn": ("sbuf", [128, 4, 4, 32], F32),
    "SUM": ("sbuf", [128, 4], F32),
    "N": ("sbuf", [128, 4], F32),
    "MSG": ("sbuf", [128, 8], F32),
    "L": ("sbuf", [128, 32], F32),
    "NA": ("sbuf", [128, 4], F32),
    "JQ": ("sbuf", [128, 16], F32),
    "T1": ("sbuf", [128, 16], F32),
    "D0": ("sbuf", [128, 20], F32),
    "D1": ("sbuf", [128, 20], F32),
    "SC": ("sbuf", [128, 20], F32),
    "SO": ("sbuf", [128, 4], F32),
    "IK": ("sbuf", [128, 4], F32),
    "KD": ("sbuf", [128, 4], F32),
    "RO": ("sbuf", [128, 4], F32),
    "KRO": ("sbuf", [128, 4], F32),
    "SR": ("sbuf", [128, 4], F32),
    "IR": ("sbuf", [128, 4], F32),
    "GF": ("sbuf", [128, 4], F32),
    "NBO": ("sbuf", [128, 4], F32),
}
SEMAPHORES = ["ld0", "ld1", "v", "s", "arr", "snt", "st"]
EPS = 0.01
NENG = 8


def rank_program(g, core, T, topo):
    rank = T.rank_of(core)
    if rank is None:
        return
    grp = [m for m in T.tables["GRP"] if rank in m][0]
    G = len(grp)
    P = G - 1
    D = 128 * G
    peers = [q for q in grp if q != rank]
    sem = T.sem
    A = AluOpType
    F = ActivationFunctionType
    vec, sca, syn = g.vector, g.scalar, g.sync
    nv, ns = [0], [0]

    def V(inst):
        inst.then_inc(sem.v, 1)
        nv[0] += 1
        return nv[0]

    def S(inst):
        inst.then_inc(sem.s, 1)
        ns[0] += 1
        return ns[0]

    def vdep():
        vec.wait_ge(sem.v, nv[0])

    def sdep():
        sca.wait_ge(sem.s, ns[0])

    def tok(buf, c):
        return buf[:, 128 * c:128 * c + 128]

    def col(buf, c):
        return buf[:, c:c + 1]

    def step(buf, k):
        return buf[:, k:20:5]

    def s_mean(c):
        return S(sca.activation(tok(T.J, c), tok(T.Tt, c), F.Identity, scale=-1.0 / 128.0, accum_out=col(T.N, c)))

    def s_square(c):
        return S(sca.activation(tok(T.J, c), tok(T.Tt, c), F.Square, bias=col(T.N, c), accum_out=col(T.MSG, 2 * c + 1)))

    mask = 0xFFFF
    for q in peers:
        mask &= topo.mask(core, T.cores[q])
    eng = [i for i in range(16) if (mask >> i) & 1][:NENG]
    emask = sum(1 << i for i in eng)

    def send(lo, hi):
        ids, dsts = [], []
        for q in peers:
            rid, pid = topo.addr(T.cores[q], core)
            slot = [m for m in grp if m != q].index(rank)
            ids.append(DstId(rid=rid, pnc=pid))
            dsts.append(T.L[:, 8 * slot + lo:8 * slot + hi])
        g.remote_dma_fused([RemoteDMATransfer(dst_ids=ids, dma_engine_mask=emask, remote_sem=sem.arr,
                                              srcs=[T.MSG[:, lo:hi]], dsts=dsts, alu_op=0)], local_sem=sem.snt)

    for h in range(2):
        for a in range(4):
            q = syn if a < 2 else sca
            q.dma_start(T.X[32 * a:32 * a + 32, :, 2 * h:2 * h + 2, :],
                        T.x[:, 128 * a + 64 * h:128 * a + 64 * h + 64]).then_inc(sem["ld%d" % h], 16)

    V(vec.memset(step(T.D0, 0), 0.0))
    V(vec.memset(step(T.D0, 2), -1.0 / G))
    V(vec.memset(step(T.D0, 3), 1.0))
    V(vec.memset(step(T.D1, 1), 0.0))
    V(vec.memset(step(T.D1, 4), 0.0))

    vec.wait_ge(sem.ld0, 64)
    v_t0 = V(vec.transpose(tok(T.Tt, 0), T.X[:, :, 0, :]))
    V(vec.transpose(tok(T.Tt, 1), T.X[:, :, 1, :]))
    sca.wait_ge(sem.v, v_t0)
    s_m0 = s_mean(0)
    sdep()
    s_sq0 = s_square(0)
    vdep()
    V(vec.tensor_reduce(col(T.SUM, 1), tok(T.Tt, 1), AxisListType.X, A.add, negate=True))
    vec.wait_ge(sem.s, s_m0)
    v_a0 = V(vec.tensor_scalar(col(T.MSG, 0), col(T.N, 0), math.sqrt(128.0), None, A.mult))
    vdep()
    v_n1 = V(vec.tensor_scalar(col(T.N, 1), col(T.SUM, 1), 1.0 / 128.0, None, A.mult))
    sca.wait_ge(sem.v, v_n1)
    s_square(1)
    g.wait_ge(sem.v, v_a0)
    g.wait_ge(sem.s, s_sq0)
    send(0, 2)
    vec.wait_ge(sem.ld1, 64)
    v_t2 = V(vec.transpose(tok(T.Tt, 2), T.X[:, :, 2, :]))
    v_t3 = V(vec.transpose(tok(T.Tt, 3), T.X[:, :, 3, :]))
    sca.wait_ge(sem.v, v_t2)
    s_m2 = s_mean(2)
    sca.wait_ge(sem.v, v_t3)
    s_m3 = s_mean(3)
    sca.wait_ge(sem.s, s_m2)
    s_square(2)
    sca.wait_ge(sem.s, s_m3)
    s_sq = s_square(3)
    vdep()
    vec.wait_ge(sem.s, s_m3)
    v_a = V(vec.tensor_scalar(T.MSG[:, 2:8:2], T.N[:, 1:4], math.sqrt(128.0), None, A.mult))
    g.wait_ge(sem.v, v_a)
    g.wait_ge(sem.s, s_sq)
    send(2, 8)
    g.wait_ge(sem.snt, 2 * len(eng))
    landed = 2 * len(eng) * P

    zo = T.L[:, 8 * P + 1:8 * G:2]
    sdep()
    S(sca.activation(T.SO[:], T.MSG[:, 1:8:2], F.Sqrt, bias=EPS, scale=1.0 / D))
    vec.wait_ge(sem.s, s_sq)
    V(vec.tensor_scalar(zo, T.MSG[:, 1:8:2], float(D * EPS), None, A.add))
    vdep()
    V(vec.reciprocal(T.IK[:], zo))
    V(vec.tensor_scalar(T.L[:, 8 * P:8 * G:2], T.MSG[:, 0:8:2], -float(P), None, A.mult))
    V(vec.tensor_scalar(T.NA[:], T.MSG[:, 0:8:2], -1.0, None, A.mult))
    vdep()
    v_kd = V(vec.tensor_scalar(T.KD[:], T.IK[:], float(D), None, A.mult))
    for c in range(4):
        V(vec.tensor_scalar(tok(T.Dd, c), tok(T.Tt, c), col(T.N, c), None, A.add))
    sdep()
    sca.wait_ge(sem.v, v_kd)
    for c in range(4):
        S(sca.activation(col(T.RO, c), col(T.SO, c), F.Identity, scale=col(T.KD, c)))
    sdep()
    s_k = S(sca.activation(T.KRO[:], T.RO[:], F.Identity, scale=1.0 / (G * math.sqrt(128.0))))
    S(sca.activation(step(T.D0, 4), T.RO[:], F.Square, scale=float(D) ** -0.5))

    sca.wait_ge(sem.arr, landed)
    s_q = 0
    for c in range(4):
        s_q = S(sca.activation(T.JQ[:, 4 * c:4 * c + P], T.L[:, 2 * c:8 * P:8], F.Square, bias=col(T.NA, c),
                               accum_out=T.D1[:, 5 * c + 3:5 * c + 4]))
    vdep()
    vec.wait_ge(sem.arr, landed)
    if G == 4:
        V(vec.tensor_tensor(T.T1[:], T.L[:, 0:16], T.L[:, 16:32], A.add))
        vdep()
        pair = T.T1
    else:
        pair = T.L
    v_t = V(vec.tensor_tensor(step(T.D1, 0), pair[:, 0:8:2], pair[:, 8:16:2], A.add))
    V(vec.tensor_tensor(step(T.D0, 1), pair[:, 0:8:2], pair[:, 8:16:2], A.add))
    V(vec.tensor_tensor(step(T.D1, 2), pair[:, 1:8:2], pair[:, 9:16:2], A.add))
    vec.wait_ge(sem.v, v_t)
    vec.wait_ge(sem.s, s_k)
    v_nbo = V(vec.tensor_tensor(T.NBO[:], step(T.D1, 0), T.KRO[:], A.mult))
    vdep()
    vec.wait_ge(sem.s, s_q)
    v_rho = V(vec.tensor_tensor_scan(T.SC[:], T.D0[:], T.D1[:], 0.0, A.mult, A.add))
    rho = step(T.SC, 4)

    def s_w(c):
        return S(sca.activation(tok(T.U, c), tok(T.Dd, c), F.Identity, bias=col(T.NBO, c), scale=col(T.RO, c)))

    sca.wait_ge(sem.v, v_nbo)
    s_w(2)
    sca.wait_ge(sem.v, v_rho)
    s_sr = S(sca.activation(T.SR[:], rho, F.Sqrt))
    s_w3 = s_w(3)
    s_w(0)
    s_w(1)
    vdep()
    v_ir = V(vec.reciprocal(T.IR[:], rho))

    sdep()
    sca.wait_ge(sem.v, v_ir)
    for c in (0, 1):
        S(sca.activation(col(T.GF, c), col(T.SR, c), F.Identity, scale=col(T.IR, c)))
    sdep()
    s_y = {}
    for c in (0, 1):
        s_y[c] = S(sca.activation(tok(T.Yt, c), tok(T.U, c), F.Identity, scale=col(T.GF, c)))
    vdep()
    vec.wait_ge(sem.s, s_sr)
    v_y = {}
    v_y[2] = V(vec.tensor_scalar(tok(T.Yt, 2), tok(T.U, 2), col(T.SR, 2), col(T.IR, 2), A.mult, A.mult))
    vec.wait_ge(sem.s, s_w3)
    v_y[3] = V(vec.tensor_scalar(tok(T.Yt, 3), tok(T.U, 3), col(T.SR, 3), col(T.IR, 3), A.mult, A.mult))
    v_first = 0
    for c in (2, 3):
        vec.wait_ge(sem.v, v_y[c])
        v_first = V(vec.transpose(T.Yn[:, :, c, :], tok(T.Yt, c)))
    v_last = 0
    for c in (0, 1):
        vec.wait_ge(sem.s, s_y[c])
        v_last = V(vec.transpose(T.Yn[:, :, c, :], tok(T.Yt, c)))

    def store(q, a, h):
        q.dma_start(T.y[:, 128 * a + 64 * h:128 * a + 64 * h + 64],
                    T.Yn[32 * a:32 * a + 32, :, 2 * h:2 * h + 2, :]).then_inc(sem.st, 16)

    syn.wait_ge(sem.v, v_first)
    for a in range(4):
        store(syn, a, 1)
    syn.wait_ge(sem.v, v_last)
    sca.wait_ge(sem.v, v_last)
    for a in range(4):
        store(syn if a < 2 else sca, a, 0)
    syn.wait_ge(sem.st, 128)
